import numpy as np
import ml_dtypes


def mxq(x, axis, fmt="e4m3"):
    dtype, down = {"e4m3": (ml_dtypes.float8_e4m3fn, 7), "e5m2": (ml_dtypes.float8_e5m2, 14)}[fmt]
    v = np.moveaxis(np.asarray(x, np.float32).astype(ml_dtypes.bfloat16).astype(np.float64), axis, -1)
    blocks = v.reshape(v.shape[:-1] + (-1, 32))
    amax = np.abs(blocks).max(-1, keepdims=True)
    byte = np.maximum(np.where(amax > 0, np.frexp(amax)[1] - 1 + 127, 0) - down, 1)
    scale = np.exp2(byte - 127.0)
    codes = (blocks / scale).astype(np.float32).astype(dtype).astype(np.float64)
    return np.moveaxis((codes * scale).reshape(v.shape), -1, axis)


WIDE = False


def mx_kscale(k, group=512):
    if not WIDE:
        return np.ones(k)
    levels = np.array([10, -10, 5, -5, 0])
    if group != 512:
        return np.exp2(np.random.permutation(np.resize(levels, k // group))).repeat(group)
    if k % 512:
        return np.exp2(np.random.permutation(np.resize(levels, k // 32))).repeat(32)
    a = np.empty((k // 512, 16))
    for p in range(k // 512):
        a[p, :8] = np.random.permutation(np.resize(levels, 8))
        for g in range(8):
            far = levels[np.abs(levels - a[p, g]) >= 10]
            a[p, g + 8] = far[np.random.randint(len(far))]
    return np.exp2(a.ravel()).repeat(32)


def f64(x):
    return np.asarray(x).astype(np.float64)


def striped(idx):
    return np.tile(np.asarray(idx).reshape(-1, 16).T, (8, 1)).astype(np.uint16)


def unstriped(offs):
    return offs[:16].T.reshape(-1).astype(np.int64)


H, KV, D, NQ, N = 4, 4, 128, 512, 512
CAP = 2.0


def setup_inputs():
    n = np.random.standard_normal
    s = mx_kscale(D, 0)[:, None]
    u = mx_kscale(N)
    t = np.random.uniform(0.5, 2.0, N) * u
    v = n((KV, N, 128))
    return {
        "qT": (n((H, D, NQ)) * s * (0.70 / np.sqrt(D))).astype(np.float32),
        "kT": (n((KV, D, N)) / s).astype(np.float32),
        "t": t.reshape(N, 1).astype(np.float32),
        "v": (v / t[:, None]).astype(np.float32),
        "gn": np.tile(np.random.uniform(0.5, 2.0, 128), (128, 1)).astype(np.float32),
    }


def reference(qT, kT, t, v, gn):
    a = mxq(f64(kT), 1, "e4m3").transpose(0, 2, 1) @ mxq(f64(qT), 1, "e4m3")
    a = CAP * np.tanh(a / CAP)
    p = 1.0 / (1.0 + np.exp(-a))
    w = p * f64(t)
    y = mxq(w, 1, "e4m3").transpose(0, 2, 1) @ mxq(f64(v), 1, "e4m3")
    y = y / 16.0
    y = y / np.sqrt(np.mean(np.square(y), -1, keepdims=True) + 1e-5) * f64(gn)[:1]
    return y

@@ -1,0 +1,249 @@
+from contextlib import ExitStack
+
+import concourse.mybir as mybir
+
+H, D, NQ, N, E = 4, 128, 512, 512, 128
+FLOPS = 2 * H * N * NQ * D + 2 * H * NQ * N * E
+
+F32 = mybir.dt.float32
+BF16 = mybir.dt.bfloat16
+U32 = mybir.dt.uint32
+U8 = mybir.dt.uint8
+FP8X4 = mybir.dt.float8_e4m3fn_x4
+ACT = mybir.ActivationFunctionType
+ALU = mybir.AluOpType
+
+P = 128
+PACK = 4
+ROWS = D // PACK
+QB = 128
+CHUNKS = NQ // QB
+TILES = CHUNKS * H
+EPS = 256 * 1e-5
+
+
+def tile_rows_a_sigmoid_cap_onorm_kernel(tc, qT, kT, t, v, gn, out):
+    nc = tc.nc
+    with ExitStack() as ctx:
+        sb = ctx.enter_context(tc.tile_pool(name="sb", bufs=1))
+        ps = ctx.enter_context(tc.psum_pool(name="ps", bufs=1))
+        ctx.enter_context(tc.manual_schedule())
+
+        def sbuf(name, shape, dtype):
+            return sb.tile(shape, dtype, name=name, align_bytes=64)
+
+        def quantize(name, src, words):
+            codes = sbuf(name + "_codes", [P, words], U32)
+            scales = sbuf(name + "_scales", [P, words], U8)
+            nc.vector.quantize_mx(out=codes[:].bitcast(FP8X4), scales=scales[:], in_=src)
+            return codes, scales
+
+        q_hbm = qT.rearrange("h (p j) n -> (h p) j n", j=PACK)
+        k_hbm = kT.rearrange("h (p j) n -> (h p) j n", j=PACK)
+        v_hbm = v.rearrange("h (s r) e -> s h (r e)", r=PACK)
+
+        q_raw = [sbuf("q_raw0", [P, PACK, QB], F32), sbuf("q_raw1", [P, PACK, QB], F32),
+                 sbuf("q_raw23", [P, PACK, 2 * QB], F32)]
+        k_raw = [sbuf("k_raw%d" % c, [P, PACK, N // 2], F32) for c in range(2)]
+        v_raw = [sbuf("v_raw%d" % c, [P, 2, PACK * E], F32) for c in range(2)]
+        t_sb = sbuf("t_sb", [P, PACK], F32)
+        gn_sb = sbuf("gn_sb", [P, E], F32)
+
+        nc.scalar.dma_start(out=t_sb[:], in_=t.rearrange("(s r) o -> s (r o)", r=PACK))
+        nc.sync.dma_start(out=q_raw[0][:], in_=q_hbm[:, :, 0:QB])
+        for c in range(2):
+            nc.sync.dma_start(out=k_raw[c][:], in_=k_hbm[:, :, c * 256:(c + 1) * 256])
+        nc.sync.dma_start(out=v_raw[0][:], in_=v_hbm[:, 0:2, :])
+        nc.sync.dma_start(out=q_raw[1][:], in_=q_hbm[:, :, QB:2 * QB])
+        nc.sync.dma_start(out=v_raw[1][:], in_=v_hbm[:, 2:4, :])
+        nc.sync.dma_start(out=q_raw[2][:], in_=q_hbm[:, :, 2 * QB:4 * QB])
+        nc.sync.dma_start(out=gn_sb[:], in_=gn)
+
+        half_t = sbuf("half_t", [P, PACK], F32)
+        nc.gpsimd.tensor_scalar(out=half_t[:], in0=t_sb[:], scalar1=0.5, scalar2=0.0, op0=ALU.mult, op1=ALU.add)
+        minus_half = sbuf("minus_half", [P, H], F32)
+        nc.gpsimd.memset(minus_half[:], -0.5)
+
+        q_bf, q_mx, v_bf, v_mx = {}, {}, {}, {}
+
+        def round_q(c):
+            src = q_raw[c][:] if c < 2 else q_raw[2][:, :, (c - 2) * QB:(c - 1) * QB]
+            q_bf[c] = sbuf("q_bf%d" % c, [P, QB * PACK], BF16)
+            nc.vector.tensor_copy(
+                out=q_bf[c][:].rearrange("p (c i j) -> p c j i", i=4, j=PACK),
+                in_=src.rearrange("p j (c i) -> p c j i", i=4))
+
+        def quant_q(c):
+            q_mx[c] = quantize("q%d" % c, q_bf[c][:], QB)
+
+        def round_v(g):
+            v_bf[g] = sbuf("v_bf%d" % g, [P, 2 * E * PACK], BF16)
+            nc.vector.tensor_copy(
+                out=v_bf[g][:].rearrange("p (h c i r) -> p h c r i", h=2, i=4, r=PACK),
+                in_=v_raw[g][:].rearrange("p h (r c i) -> p h c r i", r=PACK, i=4))
+
+        def quant_v(g):
+            v_mx[g] = quantize("v%d" % g, v_bf[g][:], 2 * E)
+
+        round_q(0)
+        quant_q(0)
+        k_bf = sbuf("k_bf", [P, N * PACK], BF16)
+        k_view = k_bf[:].rearrange("p (r s j) -> p s j r", r=PACK, j=PACK)
+        for c in range(2):
+            nc.vector.tensor_copy(
+                out=k_view[:, 64 * c:64 * (c + 1), :, :],
+                in_=k_raw[c][:].rearrange("p j (s r) -> p s j r", r=PACK))
+        k_mx = [quantize("k%d" % c, k_bf[:, 1024 * c:1024 * (c + 1)], 256) for c in range(2)]
+
+        score_bank = [ps.tile([P, PACK * QB], F32, name="score%d" % h) for h in range(H)]
+        y_bank = [ps.tile([P, CHUNKS * E], F32, name="y%d" % h) for h in range(H)]
+
+        def y_of(i):
+            c, h = divmod(i, H)
+            return y_bank[h][:, c * E:(c + 1) * E]
+
+        def scores(i):
+            c, h = divmod(i, H)
+            rows = slice(ROWS * h, ROWS * (h + 1))
+            q_codes, q_scales = q_mx[c]
+            for r in range(PACK):
+                k_codes, k_scales = k_mx[r // 2]
+                cols = slice(P * (r % 2), P * (r % 2 + 1))
+                nc.tensor.matmul_mx(
+                    out=score_bank[h][:, r * QB:(r + 1) * QB],
+                    lhsT=k_codes[rows, cols].bitcast(FP8X4), lhsT_scale=k_scales[rows, cols],
+                    rhs=q_codes[rows, :].bitcast(FP8X4), rhs_scale=q_scales[rows, :],
+                    start=True, stop=True)
+
+        capped, gated, w_bf, w_mx = {}, {}, {}, {}
+
+        def tanh_cap(i):
+            capped[i] = sbuf("capped%d" % i, [P, QB * PACK], F32)
+            nc.scalar.activation(
+                out=capped[i][:].rearrange("p (q r) -> p q r", r=PACK),
+                in_=score_bank[i % H][:].rearrange("p (r q) -> p q r", r=PACK),
+                func=ACT.Tanh, scale=0.5)
+
+        def tanh_gate(i):
+            gated[i] = sbuf("gated%d" % i, [P, QB * PACK], F32)
+            nc.scalar.activation(out=gated[i][:], in_=capped[i][:], func=ACT.Tanh)
+
+        def weigh(i):
+            w_bf[i] = sbuf("w_bf%d" % i, [P, QB * PACK], BF16)
+            nc.vector.scalar_tensor_tensor(
+                out=w_bf[i][:].rearrange("p (q r) -> p q r", r=PACK),
+                in0=gated[i][:].rearrange("p (q r) -> p q r", r=PACK), scalar=1.0,
+                in1=half_t[:, 0:PACK].unsqueeze(1).to_broadcast([P, QB, PACK]),
+                op0=ALU.add, op1=ALU.mult)
+
+        def quant_w(i):
+            w_mx[i] = quantize("w%d" % i, w_bf[i][:], QB)
+
+        def mix(i):
+            h = i % H
+            w_codes, w_scales = w_mx[i]
+            v_codes, v_scales = v_mx[h // 2]
+            cols = slice(E * (h % 2), E * (h % 2 + 1))
+            nc.tensor.matmul_mx(
+                out=y_of(i), lhsT=w_codes[:].bitcast(FP8X4), lhsT_scale=w_scales[:],
+                rhs=v_codes[:, cols].bitcast(FP8X4), rhs_scale=v_scales[:, cols],
+                start=True, stop=True)
+
+        stats = [sbuf("stats%d" % c, [P, H * 6], F32) for c in range(CHUNKS)]
+        mean_sq = [sbuf("mean_sq%d" % c, [P, H * 2], F32) for c in range(CHUNKS)]
+        half_ms = [sbuf("half_ms%d" % c, [P, H * 2], F32) for c in range(CHUNKS)]
+        ms = [sbuf("ms%d" % c, [P, H], F32) for c in range(CHUNKS)]
+        inv_rms = [sbuf("inv_rms%d" % c, [P, H], F32) for c in range(CHUNKS)]
+        result = [sbuf("result%d" % c, [P, H, E], F32) for c in range(CHUNKS)]
+
+        def moments(i):
+            c, h = divmod(i, H)
+            nc.vector.bn_stats(out=stats[c][:, 6 * h:6 * (h + 1)], in_=y_of(i))
+
+        def square_means(c, n):
+            means = stats[c][:, 1:6 * n:3]
+            nc.vector.scalar_tensor_tensor(out=mean_sq[c][:, 0:2 * n], in0=means, scalar=0.5, in1=means,
+                                           op0=ALU.mult, op1=ALU.mult)
+
+        def add_variances(c, n):
+            nc.vector.scalar_tensor_tensor(out=half_ms[c][:, 0:2 * n], in0=stats[c][:, 2:6 * n:3], scalar=1.0 / E,
+                                           in1=mean_sq[c][:, 0:2 * n], op0=ALU.mult, op1=ALU.add)
+
+        def add_halves(c, n):
+            nc.vector.scalar_tensor_tensor(out=ms[c][:, 0:n], in0=half_ms[c][:, 0:2 * n:2], scalar=EPS,
+                                           in1=half_ms[c][:, 1:2 * n:2], op0=ALU.add, op1=ALU.add)
+
+        def root_gpsimd(c):
+            nc.gpsimd.tensor_tensor(out=inv_rms[c][:], in0=ms[c][:], in1=minus_half[:], op=ALU.pow)
+
+        def normalise(i):
+            c, h = divmod(i, H)
+            nc.vector.scalar_tensor_tensor(out=result[c][:, h, :], in0=y_of(i), scalar=inv_rms[c][:, h:h + 1],
+                                           in1=gn_sb[:], op0=ALU.mult, op1=ALU.mult)
+
+        def store(c, h0, h1):
+            nc.sync.dma_start(out=out[h0:h1, c * QB:(c + 1) * QB, :].rearrange("h q e -> q h e"),
+                              in_=result[c][:, h0:h1, :])
+
+        for i in range(H):
+            scores(i)
+        tanh_cap(0)
+        round_v(0)
+        round_q(1)
+        quant_v(0)
+        quant_q(1)
+
+        last = TILES - 1
+        for i in range(TILES):
+            c, h = divmod(i, H)
+            if i + 1 < TILES:
+                tanh_cap(i + 1)
+            if i + H < TILES:
+                scores(i + H)
+            tanh_gate(i)
+            weigh(i)
+            if i == 0:
+                round_v(1)
+            if i >= 1:
+                moments(i - 1)
+            if c >= 1 and h == 1:
+                add_variances(c - 1, H)
+            if h == 2 and c + 2 < CHUNKS:
+                round_q(c + 2)
+            quant_w(i)
+            mix(i)
+            if i == 1:
+                quant_v(1)
+            if h == 3 and c + 2 < CHUNKS:
+                quant_q(c + 2)
+            if c >= 1 and h == 0:
+                square_means(c - 1, H)
+            if c >= 1 and h == 1:
+                add_halves(c - 1, H)
+                root_gpsimd(c - 1)
+                if c >= 2:
+                    for j in range(H):
+                        normalise((c - 2) * H + j)
+                    store(c - 2, 0, H)
+            if i == last - 1:
+                normalise(8)
+                normalise(9)
+
+        c = CHUNKS - 1
+        square_means(c, H - 1)
+        normalise(10)
+        add_variances(c, H - 1)
+        normalise(11)
+        store(c - 1, 0, H)
+        add_halves(c, H - 1)
+        nc.scalar.activation(out=inv_rms[c][:, 0:H - 1], in_=ms[c][:, 0:H - 1], func=ACT.Abs_reciprocal_sqrt)
+        squares = sbuf("squares", [P, E], F32)
+        sum_sq = sbuf("sum_sq", [P, 1], F32)
+        nc.scalar.activation(out=squares[:], in_=y_of(last), func=ACT.Square, accum_out=sum_sq[:])
+        nc.scalar.activation(out=inv_rms[c][:, H - 1:H], in_=sum_sq[:], func=ACT.Abs_reciprocal_sqrt,
+                             scale=1.0 / E, bias=EPS)
+        for j in range(H - 1):
+            normalise(c * H + j)
+        store(c, 0, H - 1)
+        normalise(last)
+        store(c, H - 1, H)

@@ -8,6 +8,7 @@ FLOPS = 2 * H * N * NQ * D + 2 * H * NQ * N * E
 F32 = mybir.dt.float32
 BF16 = mybir.dt.bfloat16
 U32 = mybir.dt.uint32
+I32 = mybir.dt.int32
 U8 = mybir.dt.uint8
 FP8X4 = mybir.dt.float8_e4m3fn_x4
 ACT = mybir.ActivationFunctionType
@@ -20,6 +21,10 @@ QB = 128
 CHUNKS = NQ // QB
 TILES = CHUNKS * H
 EPS = 256 * 1e-5
+EARLY = 8
+ROOT_GUESS = float(0x5F1FFFF9)
+ROOT_STEPS = ((-0.703952253, 0.703952253 * 2.38924456), (-0.5, 1.5), (-0.5, 1.5))
+NEWTON_STEPS = len(ROOT_STEPS)
 
 
 def tile_rows_a_sigmoid_cap_onorm_kernel(tc, qT, kT, t, v, gn, out):
@@ -59,22 +64,28 @@ def tile_rows_a_sigmoid_cap_onorm_kernel(tc, qT, kT, t, v, gn, out):
         nc.sync.dma_start(out=q_raw[2][:], in_=q_hbm[:, :, 2 * QB:4 * QB])
         nc.sync.dma_start(out=gn_sb[:], in_=gn)
 
-        half_t = sbuf("half_t", [P, PACK], F32)
-        nc.gpsimd.tensor_scalar(out=half_t[:], in0=t_sb[:], scalar1=0.5, scalar2=0.0, op0=ALU.mult, op1=ALU.add)
-        minus_half = sbuf("minus_half", [P, H], F32)
-        nc.gpsimd.memset(minus_half[:], -0.5)
-
         q_bf, q_mx, v_bf, v_mx = {}, {}, {}, {}
 
         def round_q(c):
-            src = q_raw[c][:] if c < 2 else q_raw[2][:, :, (c - 2) * QB:(c - 1) * QB]
             q_bf[c] = sbuf("q_bf%d" % c, [P, QB * PACK], BF16)
             nc.vector.tensor_copy(
                 out=q_bf[c][:].rearrange("p (c i j) -> p c j i", i=4, j=PACK),
-                in_=src.rearrange("p j (c i) -> p c j i", i=4))
+                in_=q_raw[c][:].rearrange("p j (c i) -> p c j i", i=4))
 
         def quant_q(c):
-            q_mx[c] = quantize("q%d" % c, q_bf[c][:], QB)
+            codes, scales = quantize("q%d" % c, q_bf[c][:], QB)
+            q_mx[c] = (codes[:], scales[:])
+
+        def round_q_late():
+            q_bf[2] = sbuf("q_bf2", [P, 2 * QB * PACK], BF16)
+            nc.vector.tensor_copy(
+                out=q_bf[2][:].rearrange("p (c u m j) -> p u j m c", c=2, m=2, j=PACK),
+                in_=q_raw[2][:].rearrange("p j (u m c) -> p u j m c", m=2, c=2))
+
+        def quant_q_late():
+            codes, scales = quantize("q2", q_bf[2][:], 2 * QB)
+            for c in range(2):
+                q_mx[2 + c] = (codes[:, c * QB:(c + 1) * QB], scales[:, c * QB:(c + 1) * QB])
 
         def round_v(g):
             v_bf[g] = sbuf("v_bf%d" % g, [P, 2 * E * PACK], BF16)
@@ -86,14 +97,20 @@ def tile_rows_a_sigmoid_cap_onorm_kernel(tc, qT, kT, t, v, gn, out):
             v_mx[g] = quantize("v%d" % g, v_bf[g][:], 2 * E)
 
         round_q(0)
+        half_t = sbuf("half_t", [P, PACK], F32)
+        nc.vector.tensor_scalar(out=half_t[:], in0=t_sb[:], scalar1=0.5, scalar2=None, op0=ALU.mult)
         quant_q(0)
-        k_bf = sbuf("k_bf", [P, N * PACK], BF16)
-        k_view = k_bf[:].rearrange("p (r s j) -> p s j r", r=PACK, j=PACK)
+        k_codes = sbuf("k_codes", [P, N], U32)
+        k_scales = sbuf("k_scales", [P, N], U8)
         for c in range(2):
+            k_bf = sbuf("k_bf%d" % c, [P, PACK, 64 * PACK], BF16)
             nc.vector.tensor_copy(
-                out=k_view[:, 64 * c:64 * (c + 1), :, :],
+                out=k_bf[:].rearrange("p r (s j) -> p s j r", j=PACK),
                 in_=k_raw[c][:].rearrange("p j (s r) -> p s j r", r=PACK))
-        k_mx = [quantize("k%d" % c, k_bf[:, 1024 * c:1024 * (c + 1)], 256) for c in range(2)]
+            for r in range(PACK):
+                cols = slice(P * r + 64 * c, P * r + 64 * (c + 1))
+                nc.vector.quantize_mx(out=k_codes[:, cols].bitcast(FP8X4), scales=k_scales[:, cols],
+                                      in_=k_bf[:, r, :])
 
         score_bank = [ps.tile([P, PACK * QB], F32, name="score%d" % h) for h in range(H)]
         y_bank = [ps.tile([P, CHUNKS * E], F32, name="y%d" % h) for h in range(H)]
@@ -107,8 +124,7 @@ def tile_rows_a_sigmoid_cap_onorm_kernel(tc, qT, kT, t, v, gn, out):
             rows = slice(ROWS * h, ROWS * (h + 1))
             q_codes, q_scales = q_mx[c]
             for r in range(PACK):
-                k_codes, k_scales = k_mx[r // 2]
-                cols = slice(P * (r % 2), P * (r % 2 + 1))
+                cols = slice(P * r, P * (r + 1))
                 nc.tensor.matmul_mx(
                     out=score_bank[h][:, r * QB:(r + 1) * QB],
                     lhsT=k_codes[rows, cols].bitcast(FP8X4), lhsT_scale=k_scales[rows, cols],
@@ -149,41 +165,67 @@ def tile_rows_a_sigmoid_cap_onorm_kernel(tc, qT, kT, t, v, gn, out):
                 rhs=v_codes[:, cols].bitcast(FP8X4), rhs_scale=v_scales[:, cols],
                 start=True, stop=True)
 
-        stats = [sbuf("stats%d" % c, [P, H * 6], F32) for c in range(CHUNKS)]
-        mean_sq = [sbuf("mean_sq%d" % c, [P, H * 2], F32) for c in range(CHUNKS)]
-        half_ms = [sbuf("half_ms%d" % c, [P, H * 2], F32) for c in range(CHUNKS)]
-        ms = [sbuf("ms%d" % c, [P, H], F32) for c in range(CHUNKS)]
-        inv_rms = [sbuf("inv_rms%d" % c, [P, H], F32) for c in range(CHUNKS)]
-        result = [sbuf("result%d" % c, [P, H, E], F32) for c in range(CHUNKS)]
+        stats = [sbuf("stats%d" % g, [P, EARLY * 6], F32) for g in range(2)]
+        mean_sq = [sbuf("mean_sq%d" % g, [P, EARLY * 2], F32) for g in range(2)]
+        half_ms = [sbuf("half_ms%d" % g, [P, EARLY * 2], F32) for g in range(2)]
+        ms = [sbuf("ms%d" % g, [P, EARLY], F32) for g in range(2)]
+        inv_rms = [sbuf("inv_rms%d" % g, [P, EARLY], F32) for g in range(2)]
+        result_early = [sbuf("result%d" % c, [P, H, E], F32) for c in range(2)]
+        result_late = [sbuf("result_late%d" % h, [P, 2, E], F32) for h in range(H)]
 
         def moments(i):
+            g, n = divmod(i, EARLY)
+            nc.vector.bn_stats(out=stats[g][:, 6 * n:6 * (n + 1)], in_=y_of(i))
+
+        def mean_square_links(g, n):
+            means = stats[g][:, 1:6 * n:3]
+            return [
+                lambda: nc.vector.scalar_tensor_tensor(
+                    out=mean_sq[g][:, 0:2 * n], in0=means, scalar=0.5, in1=means, op0=ALU.mult, op1=ALU.mult),
+                lambda: nc.vector.scalar_tensor_tensor(
+                    out=half_ms[g][:, 0:2 * n], in0=stats[g][:, 2:6 * n:3], scalar=1.0 / E,
+                    in1=mean_sq[g][:, 0:2 * n], op0=ALU.mult, op1=ALU.add),
+                lambda: nc.vector.scalar_tensor_tensor(
+                    out=ms[g][:, 0:n], in0=half_ms[g][:, 0:2 * n:2], scalar=EPS,
+                    in1=half_ms[g][:, 1:2 * n:2], op0=ALU.add, op1=ALU.add),
+            ]
+
+        def newton_step_links(n, root, better):
+            root_sq = sbuf("root_sq%d" % n, [P, EARLY], F32)
+            term = sbuf("term%d" % n, [P, EARLY], F32)
+            return [
+                lambda: nc.vector.tensor_tensor(out=root_sq[:], in0=root, in1=root, op=ALU.mult),
+                lambda: nc.vector.scalar_tensor_tensor(
+                    out=term[:], in0=root_sq[:], scalar=ROOT_STEPS[n][0], in1=ms[0][:], op0=ALU.mult, op1=ALU.mult),
+                lambda: nc.vector.scalar_tensor_tensor(
+                    out=better, in0=term[:], scalar=ROOT_STEPS[n][1], in1=root, op0=ALU.add, op1=ALU.mult),
+            ]
+
+        guess = sbuf("guess", [P, EARLY], I32)
+        chain = mean_square_links(0, EARLY)
+        chain.append(lambda: nc.vector.tensor_scalar(
+            out=guess[:], in0=ms[0][:].bitcast(I32), scalar1=-0.5, scalar2=ROOT_GUESS, op0=ALU.mult, op1=ALU.add))
+        roots = [guess[:].bitcast(F32)]
+        for n in range(NEWTON_STEPS - 1):
+            roots.append(sbuf("root%d" % n, [P, EARLY], F32)[:])
+        roots.append(inv_rms[0][:])
+        for n in range(NEWTON_STEPS):
+            chain.extend(newton_step_links(n, roots[n], roots[n + 1]))
+
+        def result_of(i):
             c, h = divmod(i, H)
-            nc.vector.bn_stats(out=stats[c][:, 6 * h:6 * (h + 1)], in_=y_of(i))
-
-        def square_means(c, n):
-            means = stats[c][:, 1:6 * n:3]
-            nc.vector.scalar_tensor_tensor(out=mean_sq[c][:, 0:2 * n], in0=means, scalar=0.5, in1=means,
-                                           op0=ALU.mult, op1=ALU.mult)
-
-        def add_variances(c, n):
-            nc.vector.scalar_tensor_tensor(out=half_ms[c][:, 0:2 * n], in0=stats[c][:, 2:6 * n:3], scalar=1.0 / E,
-                                           in1=mean_sq[c][:, 0:2 * n], op0=ALU.mult, op1=ALU.add)
-
-        def add_halves(c, n):
-            nc.vector.scalar_tensor_tensor(out=ms[c][:, 0:n], in0=half_ms[c][:, 0:2 * n:2], scalar=EPS,
-                                           in1=half_ms[c][:, 1:2 * n:2], op0=ALU.add, op1=ALU.add)
-
-        def root_gpsimd(c):
-            nc.gpsimd.tensor_tensor(out=inv_rms[c][:], in0=ms[c][:], in1=minus_half[:], op=ALU.pow)
+            return result_early[c][:, h, :] if c < 2 else result_late[h][:, c - 2, :]
 
         def normalise(i):
-            c, h = divmod(i, H)
-            nc.vector.scalar_tensor_tensor(out=result[c][:, h, :], in0=y_of(i), scalar=inv_rms[c][:, h:h + 1],
+            g, n = divmod(i, EARLY)
+            nc.vector.scalar_tensor_tensor(out=result_of(i), in0=y_of(i), scalar=inv_rms[g][:, n:n + 1],
                                            in1=gn_sb[:], op0=ALU.mult, op1=ALU.mult)
 
-        def store(c, h0, h1):
-            nc.sync.dma_start(out=out[h0:h1, c * QB:(c + 1) * QB, :].rearrange("h q e -> q h e"),
-                              in_=result[c][:, h0:h1, :])
+        def store_early(c):
+            nc.sync.dma_start(out=out[:, c * QB:(c + 1) * QB, :].rearrange("h q e -> q h e"), in_=result_early[c][:])
+
+        def store_late(h):
+            nc.sync.dma_start(out=out[h, 2 * QB:4 * QB, :].rearrange("(p c) e -> p c e", c=2), in_=result_late[h][:])
 
         for i in range(H):
             scores(i)
@@ -192,58 +234,62 @@ def tile_rows_a_sigmoid_cap_onorm_kernel(tc, qT, kT, t, v, gn, out):
         round_q(1)
         quant_v(0)
         quant_q(1)
+        round_v(1)
 
         last = TILES - 1
-        for i in range(TILES):
-            c, h = divmod(i, H)
-            if i + 1 < TILES:
-                tanh_cap(i + 1)
+        for i in range(last):
+            links = chain[max(0, 3 * (i - EARLY - 1) - 2):max(0, 3 * (i - EARLY - 1) + 1)]
+            tanh_cap(i + 1)
             if i + H < TILES:
                 scores(i + H)
             tanh_gate(i)
             weigh(i)
+            if len(links) == 3:
+                links[0]()
             if i == 0:
-                round_v(1)
-            if i >= 1:
-                moments(i - 1)
-            if c >= 1 and h == 1:
-                add_variances(c - 1, H)
-            if h == 2 and c + 2 < CHUNKS:
-                round_q(c + 2)
-            quant_w(i)
-            mix(i)
-            if i == 1:
                 quant_v(1)
-            if h == 3 and c + 2 < CHUNKS:
-                quant_q(c + 2)
-            if c >= 1 and h == 0:
-                square_means(c - 1, H)
-            if c >= 1 and h == 1:
-                add_halves(c - 1, H)
-                root_gpsimd(c - 1)
-                if c >= 2:
-                    for j in range(H):
-                        normalise((c - 2) * H + j)
-                    store(c - 2, 0, H)
+            else:
+                quant_w(i - 1)
+                mix(i - 1)
+            if len(links) == 3:
+                links[1]()
+            if i == 1:
+                round_q_late()
+            if i >= 2:
+                moments(i - 2)
+            if i == 2:
+                quant_q_late()
+            if links:
+                links[-1]()
             if i == last - 1:
-                normalise(8)
-                normalise(9)
+                for j in range(H):
+                    normalise(j)
+                store_early(0)
 
-        c = CHUNKS - 1
-        square_means(c, H - 1)
-        normalise(10)
-        add_variances(c, H - 1)
-        normalise(11)
-        store(c - 1, 0, H)
-        add_halves(c, H - 1)
-        nc.scalar.activation(out=inv_rms[c][:, 0:H - 1], in_=ms[c][:, 0:H - 1], func=ACT.Abs_reciprocal_sqrt)
+        tanh_gate(last)
+        quant_w(last - 1)
+        mix(last - 1)
+        moments(last - 2)
+        weigh(last)
+        normalise(4)
+        normalise(5)
+        quant_w(last)
+        mix(last)
+        moments(last - 1)
+        links = mean_square_links(1, EARLY - 1)
+        links[0]()
+        normalise(6)
+        links[1]()
+        normalise(7)
+        store_early(1)
+        links[2]()
+        nc.scalar.activation(out=inv_rms[1][:, 0:EARLY - 1], in_=ms[1][:, 0:EARLY - 1], func=ACT.Abs_reciprocal_sqrt)
         squares = sbuf("squares", [P, E], F32)
         sum_sq = sbuf("sum_sq", [P, 1], F32)
         nc.scalar.activation(out=squares[:], in_=y_of(last), func=ACT.Square, accum_out=sum_sq[:])
-        nc.scalar.activation(out=inv_rms[c][:, H - 1:H], in_=sum_sq[:], func=ACT.Abs_reciprocal_sqrt,
+        nc.scalar.activation(out=inv_rms[1][:, EARLY - 1:EARLY], in_=sum_sq[:], func=ACT.Abs_reciprocal_sqrt,
                              scale=1.0 / E, bias=EPS)
-        for j in range(H - 1):
-            normalise(c * H + j)
-        store(c, 0, H - 1)
-        normalise(last)
-        store(c, H - 1, H)
+        for h in range(H):
+            normalise(EARLY + h)
+            normalise(EARLY + H + h)
+            store_late(h)

@@ -54,11 +54,11 @@ def tile_rows_a_sigmoid_cap_onorm_kernel(tc, qT, kT, t, v, gn, out):
         t_sb = sbuf("t_sb", [P, PACK], F32)
         gn_sb = sbuf("gn_sb", [P, E], F32)
 
-        nc.scalar.dma_start(out=t_sb[:], in_=t.rearrange("(s r) o -> s (r o)", r=PACK))
         nc.sync.dma_start(out=q_raw[0][:], in_=q_hbm[:, :, 0:QB])
         for c in range(2):
             nc.sync.dma_start(out=k_raw[c][:], in_=k_hbm[:, :, c * 256:(c + 1) * 256])
         nc.sync.dma_start(out=v_raw[0][:], in_=v_hbm[:, 0:2, :])
+        nc.sync.dma_start(out=t_sb[:], in_=t.rearrange("(s r) o -> s (r o)", r=PACK))
         nc.sync.dma_start(out=q_raw[1][:], in_=q_hbm[:, :, QB:2 * QB])
         nc.sync.dma_start(out=v_raw[1][:], in_=v_hbm[:, 2:4, :])
         nc.sync.dma_start(out=q_raw[2][:], in_=q_hbm[:, :, 2 * QB:4 * QB])
@@ -97,8 +97,6 @@ def tile_rows_a_sigmoid_cap_onorm_kernel(tc, qT, kT, t, v, gn, out):
             v_mx[g] = quantize("v%d" % g, v_bf[g][:], 2 * E)
 
         round_q(0)
-        half_t = sbuf("half_t", [P, PACK], F32)
-        nc.vector.tensor_scalar(out=half_t[:], in0=t_sb[:], scalar1=0.5, scalar2=None, op0=ALU.mult)
         quant_q(0)
         k_codes = sbuf("k_codes", [P, N], U32)
         k_scales = sbuf("k_scales", [P, N], U8)
@@ -119,30 +117,33 @@ def tile_rows_a_sigmoid_cap_onorm_kernel(tc, qT, kT, t, v, gn, out):
             c, h = divmod(i, H)
             return y_bank[h][:, c * E:(c + 1) * E]
 
-        def scores(i):
-            c, h = divmod(i, H)
-            rows = slice(ROWS * h, ROWS * (h + 1))
-            q_codes, q_scales = q_mx[c]
+        def scores(*tiles):
             for r in range(PACK):
                 cols = slice(P * r, P * (r + 1))
-                nc.tensor.matmul_mx(
-                    out=score_bank[h][:, r * QB:(r + 1) * QB],
-                    lhsT=k_codes[rows, cols].bitcast(FP8X4), lhsT_scale=k_scales[rows, cols],
-                    rhs=q_codes[rows, :].bitcast(FP8X4), rhs_scale=q_scales[rows, :],
-                    start=True, stop=True)
+                for i in tiles:
+                    c, h = divmod(i, H)
+                    rows = slice(ROWS * h, ROWS * (h + 1))
+                    q_codes, q_scales = q_mx[c]
+                    nc.tensor.matmul_mx(
+                        out=score_bank[h][:, r * QB:(r + 1) * QB],
+                        lhsT=k_codes[rows, cols].bitcast(FP8X4), lhsT_scale=k_scales[rows, cols],
+                        rhs=q_codes[rows, :].bitcast(FP8X4), rhs_scale=q_scales[rows, :],
+                        start=True, stop=True)
 
         capped, gated, w_bf, w_mx = {}, {}, {}, {}
 
         def tanh_cap(i):
             capped[i] = sbuf("capped%d" % i, [P, QB * PACK], F32)
             nc.scalar.activation(
-                out=capped[i][:].rearrange("p (q r) -> p q r", r=PACK),
-                in_=score_bank[i % H][:].rearrange("p (r q) -> p q r", r=PACK),
+                out=capped[i][:].rearrange("p (a q b) -> p a q b", a=2, b=2),
+                in_=score_bank[i % H][:].rearrange("p (a b q) -> p a q b", a=2, b=2),
                 func=ACT.Tanh, scale=0.5)
 
         def tanh_gate(i):
             gated[i] = sbuf("gated%d" % i, [P, QB * PACK], F32)
-            nc.scalar.activation(out=gated[i][:], in_=capped[i][:], func=ACT.Tanh)
+            nc.scalar.activation(
+                out=gated[i][:].rearrange("p (q a b) -> p q a b", a=2, b=2),
+                in_=capped[i][:].rearrange("p (a q b) -> p q a b", a=2, b=2), func=ACT.Tanh)
 
         def weigh(i):
             w_bf[i] = sbuf("w_bf%d" % i, [P, QB * PACK], BF16)
@@ -227,11 +228,14 @@ def tile_rows_a_sigmoid_cap_onorm_kernel(tc, qT, kT, t, v, gn, out):
         def store_late(h):
             nc.sync.dma_start(out=out[h, 2 * QB:4 * QB, :].rearrange("(p c) e -> p c e", c=2), in_=result_late[h][:])
 
-        for i in range(H):
-            scores(i)
+        scores(0)
+        scores(1)
+        scores(2, 3)
         tanh_cap(0)
         round_v(0)
         round_q(1)
+        half_t = sbuf("half_t", [P, PACK], F32)
+        nc.vector.tensor_scalar(out=half_t[:], in0=t_sb[:], scalar1=0.5, scalar2=None, op0=ALU.mult)
         quant_v(0)
         quant_q(1)
         round_v(1)
@@ -240,8 +244,8 @@ def tile_rows_a_sigmoid_cap_onorm_kernel(tc, qT, kT, t, v, gn, out):
         for i in range(last):
             links = chain[max(0, 3 * (i - EARLY - 1) - 2):max(0, 3 * (i - EARLY - 1) + 1)]
             tanh_cap(i + 1)
-            if i + H < TILES:
-                scores(i + H)
+            if i % 2 == 0 and i + H < TILES:
+                scores(i + H, i + H + 1)
             tanh_gate(i)
             weigh(i)
             if len(links) == 3:

@@ -1,3 +1,4 @@
+import math
 from contextlib import ExitStack
 
 import concourse.mybir as mybir
@@ -18,13 +19,22 @@ P = 128
 PACK = 4
 ROWS = D // PACK
 QB = 128
-CHUNKS = NQ // QB
-TILES = CHUNKS * H
+TILES = H * NQ // QB
+PAIRS = TILES // 2
+KEY_HALF = N // 2
+RUN = 4
 EPS = 256 * 1e-5
-EARLY = 8
+
+EARLY = 4
+FINAL = 6
+MIDDLE = TILES - EARLY - FINAL
+
 ROOT_GUESS = float(0x5F1FFFF9)
-ROOT_STEPS = ((-0.703952253, 0.703952253 * 2.38924456), (-0.5, 1.5), (-0.5, 1.5))
-NEWTON_STEPS = len(ROOT_STEPS)
+ROOT_STEPS = (
+    (-0.703952253, 0.703952253 * 2.38924456),
+    (-0.5, 1.5),
+    (-0.5 * math.sqrt(E), 1.5 * math.sqrt(E)),
+)
 
 
 def tile_rows_a_sigmoid_cap_onorm_kernel(tc, qT, kT, t, v, gn, out):
@@ -48,15 +58,15 @@ def tile_rows_a_sigmoid_cap_onorm_kernel(tc, qT, kT, t, v, gn, out):
         v_hbm = v.rearrange("h (s r) e -> s h (r e)", r=PACK)
 
         q_raw = [sbuf("q_raw0", [P, PACK, QB], F32), sbuf("q_raw1", [P, PACK, QB], F32),
-                 sbuf("q_raw23", [P, PACK, 2 * QB], F32)]
-        k_raw = [sbuf("k_raw%d" % c, [P, PACK, N // 2], F32) for c in range(2)]
-        v_raw = [sbuf("v_raw%d" % c, [P, 2, PACK * E], F32) for c in range(2)]
+                 sbuf("q_raw2", [P, PACK, 2 * QB], F32)]
+        k_raw = [sbuf("k_raw%d" % half, [P, PACK, KEY_HALF], F32) for half in range(2)]
+        v_raw = [sbuf("v_raw%d" % g, [P, 2, PACK * E], F32) for g in range(2)]
         t_sb = sbuf("t_sb", [P, PACK], F32)
         gn_sb = sbuf("gn_sb", [P, E], F32)
 
         nc.sync.dma_start(out=q_raw[0][:], in_=q_hbm[:, :, 0:QB])
-        for c in range(2):
-            nc.sync.dma_start(out=k_raw[c][:], in_=k_hbm[:, :, c * 256:(c + 1) * 256])
+        for half in range(2):
+            nc.sync.dma_start(out=k_raw[half][:], in_=k_hbm[:, :, half * KEY_HALF:(half + 1) * KEY_HALF])
         nc.sync.dma_start(out=v_raw[0][:], in_=v_hbm[:, 0:2, :])
         nc.sync.dma_start(out=t_sb[:], in_=t.rearrange("(s r) o -> s (r o)", r=PACK))
         nc.sync.dma_start(out=q_raw[1][:], in_=q_hbm[:, :, QB:2 * QB])
@@ -66,56 +76,50 @@ def tile_rows_a_sigmoid_cap_onorm_kernel(tc, qT, kT, t, v, gn, out):
 
         q_bf, q_mx, v_bf, v_mx = {}, {}, {}, {}
 
-        def round_q(c):
-            q_bf[c] = sbuf("q_bf%d" % c, [P, QB * PACK], BF16)
+        def round_q(first):
+            q_bf[first] = sbuf("q_bf%d" % first, [P, q_raw[first].shape[2] * PACK], BF16)
             nc.vector.tensor_copy(
-                out=q_bf[c][:].rearrange("p (c i j) -> p c j i", i=4, j=PACK),
-                in_=q_raw[c][:].rearrange("p j (c i) -> p c j i", i=4))
+                out=q_bf[first][:].rearrange("p (m x j) -> p m j x", x=RUN, j=PACK),
+                in_=q_raw[first][:].rearrange("p j (m x) -> p m j x", x=RUN))
 
-        def quant_q(c):
-            codes, scales = quantize("q%d" % c, q_bf[c][:], QB)
-            q_mx[c] = (codes[:], scales[:])
-
-        def round_q_late():
-            q_bf[2] = sbuf("q_bf2", [P, 2 * QB * PACK], BF16)
-            nc.vector.tensor_copy(
-                out=q_bf[2][:].rearrange("p (c u m j) -> p u j m c", c=2, m=2, j=PACK),
-                in_=q_raw[2][:].rearrange("p j (u m c) -> p u j m c", m=2, c=2))
-
-        def quant_q_late():
-            codes, scales = quantize("q2", q_bf[2][:], 2 * QB)
-            for c in range(2):
-                q_mx[2 + c] = (codes[:, c * QB:(c + 1) * QB], scales[:, c * QB:(c + 1) * QB])
+        def quantize_q(first):
+            width = q_raw[first].shape[2]
+            codes, scales = quantize("q%d" % first, q_bf[first][:], width)
+            for c in range(width // QB):
+                q_mx[first + c] = (codes[:, c * QB:(c + 1) * QB], scales[:, c * QB:(c + 1) * QB])
 
         def round_v(g):
             v_bf[g] = sbuf("v_bf%d" % g, [P, 2 * E * PACK], BF16)
             nc.vector.tensor_copy(
-                out=v_bf[g][:].rearrange("p (h c i r) -> p h c r i", h=2, i=4, r=PACK),
-                in_=v_raw[g][:].rearrange("p h (r c i) -> p h c r i", r=PACK, i=4))
+                out=v_bf[g][:].rearrange("p (u m x r) -> p u m r x", u=2, x=RUN, r=PACK),
+                in_=v_raw[g][:].rearrange("p u (r m x) -> p u m r x", r=PACK, x=RUN))
 
-        def quant_v(g):
+        def quantize_v(g):
             v_mx[g] = quantize("v%d" % g, v_bf[g][:], 2 * E)
 
         round_q(0)
-        quant_q(0)
+        quantize_q(0)
+
         k_codes = sbuf("k_codes", [P, N], U32)
         k_scales = sbuf("k_scales", [P, N], U8)
-        for c in range(2):
-            k_bf = sbuf("k_bf%d" % c, [P, PACK, 64 * PACK], BF16)
-            nc.vector.tensor_copy(
-                out=k_bf[:].rearrange("p r (s j) -> p s j r", j=PACK),
-                in_=k_raw[c][:].rearrange("p j (s r) -> p s j r", r=PACK))
+        half_cols = KEY_HALF // PACK
+        for half in range(2):
+            k_bf = [sbuf("k_bf%d%d" % (half, a), [P, 2, half_cols * PACK], BF16) for a in range(2)]
+            for a, copy in enumerate((nc.vector.tensor_copy, nc.scalar.copy)):
+                copy(out=k_bf[a][:].rearrange("p b (s j) -> p s j b", j=PACK),
+                     in_=k_raw[half][:].rearrange("p j (s r) -> p s j r", r=PACK)[:, :, :, 2 * a:2 * a + 2])
             for r in range(PACK):
-                cols = slice(P * r + 64 * c, P * r + 64 * (c + 1))
+                cols = slice(P * r + half_cols * half, P * r + half_cols * (half + 1))
                 nc.vector.quantize_mx(out=k_codes[:, cols].bitcast(FP8X4), scales=k_scales[:, cols],
-                                      in_=k_bf[:, r, :])
+                                      in_=k_bf[r // 2][:, r % 2, :])
 
         score_bank = [ps.tile([P, PACK * QB], F32, name="score%d" % h) for h in range(H)]
-        y_bank = [ps.tile([P, CHUNKS * E], F32, name="y%d" % h) for h in range(H)]
+        y_bank = [ps.tile([P, 4 * E], F32, name="y%d" % n) for n in range(PAIRS // 2)]
 
-        def y_of(i):
-            c, h = divmod(i, H)
-            return y_bank[h][:, c * E:(c + 1) * E]
+        def y_of(i, tiles=1):
+            pair = i // 2
+            first = 2 * (pair // (PAIRS // 2)) + i % 2
+            return y_bank[min(pair, PAIRS - 1 - pair)][:, first * E:(first + tiles) * E]
 
         def scores(*tiles):
             for r in range(PACK):
@@ -130,7 +134,7 @@ def tile_rows_a_sigmoid_cap_onorm_kernel(tc, qT, kT, t, v, gn, out):
                         rhs=q_codes[rows, :].bitcast(FP8X4), rhs_scale=q_scales[rows, :],
                         start=True, stop=True)
 
-        capped, gated, w_bf, w_mx = {}, {}, {}, {}
+        capped, gated, w_bf = {}, {}, {}
 
         def tanh_cap(i):
             capped[i] = sbuf("capped%d" % i, [P, QB * PACK], F32)
@@ -145,88 +149,110 @@ def tile_rows_a_sigmoid_cap_onorm_kernel(tc, qT, kT, t, v, gn, out):
                 out=gated[i][:].rearrange("p (q a b) -> p q a b", a=2, b=2),
                 in_=capped[i][:].rearrange("p (a q b) -> p q a b", a=2, b=2), func=ACT.Tanh)
 
+        half_t = sbuf("half_t", [P, PACK], F32)
+
         def weigh(i):
-            w_bf[i] = sbuf("w_bf%d" % i, [P, QB * PACK], BF16)
+            if i % 2 == 0:
+                w_bf[i // 2] = sbuf("w_bf%d" % i, [P, 2 * QB * PACK], BF16)
+            cols = slice(QB * PACK * (i % 2), QB * PACK * (i % 2 + 1))
             nc.vector.scalar_tensor_tensor(
-                out=w_bf[i][:].rearrange("p (q r) -> p q r", r=PACK),
+                out=w_bf[i // 2][:, cols].rearrange("p (q r) -> p q r", r=PACK),
                 in0=gated[i][:].rearrange("p (q r) -> p q r", r=PACK), scalar=1.0,
                 in1=half_t[:, 0:PACK].unsqueeze(1).to_broadcast([P, QB, PACK]),
                 op0=ALU.add, op1=ALU.mult)
 
-        def quant_w(i):
-            w_mx[i] = quantize("w%d" % i, w_bf[i][:], QB)
+        def mix(pair):
+            w_codes, w_scales = quantize("w%d" % pair, w_bf[pair][:], 2 * QB)
+            v_codes, v_scales = v_mx[pair % 2]
+            for u in range(2):
+                cols = slice(QB * u, QB * (u + 1))
+                nc.tensor.matmul_mx(
+                    out=y_of(2 * pair + u), lhsT=w_codes[:, cols].bitcast(FP8X4), lhsT_scale=w_scales[:, cols],
+                    rhs=v_codes[:, cols].bitcast(FP8X4), rhs_scale=v_scales[:, cols],
+                    start=True, stop=True)
 
-        def mix(i):
-            h = i % H
-            w_codes, w_scales = w_mx[i]
-            v_codes, v_scales = v_mx[h // 2]
-            cols = slice(E * (h % 2), E * (h % 2 + 1))
-            nc.tensor.matmul_mx(
-                out=y_of(i), lhsT=w_codes[:].bitcast(FP8X4), lhsT_scale=w_scales[:],
-                rhs=v_codes[:, cols].bitcast(FP8X4), rhs_scale=v_scales[:, cols],
-                start=True, stop=True)
+        sizes = (EARLY, MIDDLE, FINAL)
+        stats = [sbuf("stats%d" % g, [P, 3 * sizes[g]], F32) for g in range(2)]
+        mean_sq = [sbuf("mean_sq%d" % g, [P, sizes[g]], F32) for g in range(2)]
+        sum_sq = [sbuf("sum_sq%d" % g, [P, sizes[g]], F32) for g in range(3)]
+        inv_rms = [sbuf("inv_rms%d" % g, [P, sizes[g]], F32) for g in range(3)]
 
-        stats = [sbuf("stats%d" % g, [P, EARLY * 6], F32) for g in range(2)]
-        mean_sq = [sbuf("mean_sq%d" % g, [P, EARLY * 2], F32) for g in range(2)]
-        half_ms = [sbuf("half_ms%d" % g, [P, EARLY * 2], F32) for g in range(2)]
-        ms = [sbuf("ms%d" % g, [P, EARLY], F32) for g in range(2)]
-        inv_rms = [sbuf("inv_rms%d" % g, [P, EARLY], F32) for g in range(2)]
-        result_early = [sbuf("result%d" % c, [P, H, E], F32) for c in range(2)]
-        result_late = [sbuf("result_late%d" % h, [P, 2, E], F32) for h in range(H)]
+        def group_of(i):
+            if i < EARLY:
+                return 0, i
+            if i < EARLY + MIDDLE:
+                return 1, i - EARLY
+            return 2, i - EARLY - MIDDLE
 
-        def moments(i):
-            g, n = divmod(i, EARLY)
-            nc.vector.bn_stats(out=stats[g][:, 6 * n:6 * (n + 1)], in_=y_of(i))
+        def moments(pair):
+            g, n = group_of(2 * pair)
+            nc.vector.bn_stats(out=stats[g][:, 3 * n:3 * n + 6],
+                               in_=y_of(2 * pair, 2).rearrange("p (u e) -> p e u", u=2))
 
-        def mean_square_links(g, n):
-            means = stats[g][:, 1:6 * n:3]
+        def sum_sq_links(g, addend):
+            means = stats[g][:, 1:3 * sizes[g]:3]
             return [
                 lambda: nc.vector.scalar_tensor_tensor(
-                    out=mean_sq[g][:, 0:2 * n], in0=means, scalar=0.5, in1=means, op0=ALU.mult, op1=ALU.mult),
+                    out=mean_sq[g][:], in0=means, scalar=float(E), in1=means, op0=ALU.mult, op1=ALU.mult),
                 lambda: nc.vector.scalar_tensor_tensor(
-                    out=half_ms[g][:, 0:2 * n], in0=stats[g][:, 2:6 * n:3], scalar=1.0 / E,
-                    in1=mean_sq[g][:, 0:2 * n], op0=ALU.mult, op1=ALU.add),
-                lambda: nc.vector.scalar_tensor_tensor(
-                    out=ms[g][:, 0:n], in0=half_ms[g][:, 0:2 * n:2], scalar=EPS,
-                    in1=half_ms[g][:, 1:2 * n:2], op0=ALU.add, op1=ALU.add),
+                    out=sum_sq[g][:], in0=stats[g][:, 2:3 * sizes[g]:3], scalar=addend, in1=mean_sq[g][:],
+                    op0=ALU.add, op1=ALU.add),
             ]
 
-        def newton_step_links(n, root, better):
+        def root_step_links(n, root, better):
             root_sq = sbuf("root_sq%d" % n, [P, EARLY], F32)
             term = sbuf("term%d" % n, [P, EARLY], F32)
+            factor, addend = ROOT_STEPS[n]
             return [
                 lambda: nc.vector.tensor_tensor(out=root_sq[:], in0=root, in1=root, op=ALU.mult),
                 lambda: nc.vector.scalar_tensor_tensor(
-                    out=term[:], in0=root_sq[:], scalar=ROOT_STEPS[n][0], in1=ms[0][:], op0=ALU.mult, op1=ALU.mult),
+                    out=term[:], in0=root_sq[:], scalar=factor, in1=sum_sq[0][:], op0=ALU.mult, op1=ALU.mult),
                 lambda: nc.vector.scalar_tensor_tensor(
-                    out=better, in0=term[:], scalar=ROOT_STEPS[n][1], in1=root, op0=ALU.add, op1=ALU.mult),
+                    out=better, in0=term[:], scalar=addend, in1=root, op0=ALU.add, op1=ALU.mult),
             ]
 
         guess = sbuf("guess", [P, EARLY], I32)
-        chain = mean_square_links(0, EARLY)
-        chain.append(lambda: nc.vector.tensor_scalar(
-            out=guess[:], in0=ms[0][:].bitcast(I32), scalar1=-0.5, scalar2=ROOT_GUESS, op0=ALU.mult, op1=ALU.add))
+        early_roots = sum_sq_links(0, E * EPS)
+        early_roots.append(lambda: nc.vector.tensor_scalar(
+            out=guess[:], in0=sum_sq[0][:].bitcast(I32), scalar1=-0.5, scalar2=ROOT_GUESS,
+            op0=ALU.mult, op1=ALU.add))
         roots = [guess[:].bitcast(F32)]
-        for n in range(NEWTON_STEPS - 1):
+        for n in range(len(ROOT_STEPS) - 1):
             roots.append(sbuf("root%d" % n, [P, EARLY], F32)[:])
         roots.append(inv_rms[0][:])
-        for n in range(NEWTON_STEPS):
-            chain.extend(newton_step_links(n, roots[n], roots[n + 1]))
+        for n in range(len(ROOT_STEPS)):
+            early_roots.extend(root_step_links(n, roots[n], roots[n + 1]))
 
-        def result_of(i):
-            c, h = divmod(i, H)
-            return result_early[c][:, h, :] if c < 2 else result_late[h][:, c - 2, :]
+        squares = sbuf("squares", [P, E], F32)
 
-        def normalise(i):
-            g, n = divmod(i, EARLY)
-            nc.vector.scalar_tensor_tensor(out=result_of(i), in0=y_of(i), scalar=inv_rms[g][:, n:n + 1],
-                                           in1=gn_sb[:], op0=ALU.mult, op1=ALU.mult)
+        def sum_squares(i):
+            g, n = group_of(i)
+            nc.scalar.activation(out=squares[:], in_=y_of(i), func=ACT.Square, accum_out=sum_sq[g][:, n:n + 1])
 
-        def store_early(c):
-            nc.sync.dma_start(out=out[:, c * QB:(c + 1) * QB, :].rearrange("h q e -> q h e"), in_=result_early[c][:])
+        def inverse_root(g, cols):
+            nc.scalar.activation(out=inv_rms[g][:, cols], in_=sum_sq[g][:, cols], func=ACT.Abs_reciprocal_sqrt,
+                                 scale=1.0 / E, bias=EPS)
 
-        def store_late(h):
-            nc.sync.dma_start(out=out[h, 2 * QB:4 * QB, :].rearrange("(p c) e -> p c e", c=2), in_=result_late[h][:])
+        result = [sbuf("result%d" % pair, [P, 2, E], F32) for pair in range(PAIRS)]
+
+        def finish(i):
+            g, n = group_of(i)
+            nc.vector.scalar_tensor_tensor(
+                out=result[i // 2][:, i % 2, :], in0=y_of(i), scalar=inv_rms[g][:, n:n + 1], in1=gn_sb[:],
+                op0=ALU.mult, op1=ALU.mult)
+            if i % 2 == 1:
+                c, h = divmod(i - 1, H)
+                nc.sync.dma_start(out=out[h:h + 2, c * QB:(c + 1) * QB, :].rearrange("h q e -> q h e"),
+                                  in_=result[i // 2][:])
+
+        middle_sums = sum_sq_links(1, 0.0)
+        small_work = early_roots + [lambda: finish(2), middle_sums[0], lambda: finish(3), middle_sums[1],
+                                    lambda: finish(0)]
+        first_gap = 2 * (EARLY + 1) + 1
+
+        def fill(gap):
+            if 0 <= gap - first_gap < len(small_work):
+                small_work[gap - first_gap]()
 
         scores(0)
         scores(1)
@@ -234,66 +260,42 @@ def tile_rows_a_sigmoid_cap_onorm_kernel(tc, qT, kT, t, v, gn, out):
         tanh_cap(0)
         round_v(0)
         round_q(1)
-        half_t = sbuf("half_t", [P, PACK], F32)
         nc.vector.tensor_scalar(out=half_t[:], in0=t_sb[:], scalar1=0.5, scalar2=None, op0=ALU.mult)
-        quant_v(0)
-        quant_q(1)
+        quantize_v(0)
+        quantize_q(1)
         round_v(1)
 
         last = TILES - 1
         for i in range(last):
-            links = chain[max(0, 3 * (i - EARLY - 1) - 2):max(0, 3 * (i - EARLY - 1) + 1)]
             tanh_cap(i + 1)
             if i % 2 == 0 and i + H < TILES:
                 scores(i + H, i + H + 1)
             tanh_gate(i)
             weigh(i)
-            if len(links) == 3:
-                links[0]()
+            fill(2 * i)
             if i == 0:
-                quant_v(1)
-            else:
-                quant_w(i - 1)
-                mix(i - 1)
-            if len(links) == 3:
-                links[1]()
-            if i == 1:
-                round_q_late()
-            if i >= 2:
-                moments(i - 2)
+                quantize_v(1)
+            elif i == 1:
+                round_q(2)
+            elif i % 2 == 0:
+                mix(i // 2 - 1)
+            elif i - 3 < EARLY + MIDDLE:
+                moments((i - 3) // 2)
             if i == 2:
-                quant_q_late()
-            if links:
-                links[-1]()
-            if i == last - 1:
-                for j in range(H):
-                    normalise(j)
-                store_early(0)
+                quantize_q(2)
+            fill(2 * i + 1)
 
         tanh_gate(last)
-        quant_w(last - 1)
-        mix(last - 1)
-        moments(last - 2)
         weigh(last)
-        normalise(4)
-        normalise(5)
-        quant_w(last)
-        mix(last)
-        moments(last - 1)
-        links = mean_square_links(1, EARLY - 1)
-        links[0]()
-        normalise(6)
-        links[1]()
-        normalise(7)
-        store_early(1)
-        links[2]()
-        nc.scalar.activation(out=inv_rms[1][:, 0:EARLY - 1], in_=ms[1][:, 0:EARLY - 1], func=ACT.Abs_reciprocal_sqrt)
-        squares = sbuf("squares", [P, E], F32)
-        sum_sq = sbuf("sum_sq", [P, 1], F32)
-        nc.scalar.activation(out=squares[:], in_=y_of(last), func=ACT.Square, accum_out=sum_sq[:])
-        nc.scalar.activation(out=inv_rms[1][:, EARLY - 1:EARLY], in_=sum_sq[:], func=ACT.Abs_reciprocal_sqrt,
-                             scale=1.0 / E, bias=EPS)
-        for h in range(H):
-            normalise(EARLY + h)
-            normalise(EARLY + H + h)
-            store_late(h)
+        finish(1)
+        mix(PAIRS - 1)
+
+        inverse_root(1, slice(0, MIDDLE))
+        for cols in (slice(0, FINAL - 2), slice(FINAL - 2, FINAL)):
+            for n in range(cols.start, cols.stop):
+                sum_squares(EARLY + MIDDLE + n)
+            inverse_root(2, cols)
+
+        for pair in (3, 4, 2, 5, 6, 7):
+            finish(2 * pair)
+            finish(2 * pair + 1)

@@ -135,29 +135,33 @@ def tile_rows_a_sigmoid_cap_onorm_kernel(tc, qT, kT, t, v, gn, out):
                         start=True, stop=True)
 
         capped, gated, w_bf = {}, {}, {}
-
-        def tanh_cap(i):
-            capped[i] = sbuf("capped%d" % i, [P, QB * PACK], F32)
-            nc.scalar.activation(
-                out=capped[i][:].rearrange("p (a q b) -> p a q b", a=2, b=2),
-                in_=score_bank[i % H][:].rearrange("p (a b q) -> p a q b", a=2, b=2),
-                func=ACT.Tanh, scale=0.5)
-
-        def tanh_gate(i):
-            gated[i] = sbuf("gated%d" % i, [P, QB * PACK], F32)
-            nc.scalar.activation(
-                out=gated[i][:].rearrange("p (q a b) -> p q a b", a=2, b=2),
-                in_=capped[i][:].rearrange("p (a q b) -> p q a b", a=2, b=2), func=ACT.Tanh)
-
+        for pair in range(PAIRS):
+            capped[pair] = sbuf("capped%d" % pair, [P, 2 * QB * PACK], F32)
+            gated[pair] = sbuf("gated%d" % pair, [P, 2 * QB * PACK], F32)
+            w_bf[pair] = sbuf("w_bf%d" % pair, [P, 2 * QB * PACK], BF16)
         half_t = sbuf("half_t", [P, PACK], F32)
 
+        def queries_of(i, tiles=1):
+            return slice(QB * (i % 2), QB * (i % 2 + tiles))
+
+        def tanh_cap(i):
+            nc.scalar.activation(
+                out=capped[i // 2][:].rearrange("p (a m b) -> p a m b", a=2, b=2)[:, :, queries_of(i), :],
+                in_=score_bank[i % H][:].rearrange("p (a b q) -> p a q b", a=2, b=2),
+                func=ACT.Tanh, scale=0.5)
+            if i + H < TILES:
+                scores(i + H)
+
+        def tanh_gate(i, tiles):
+            nc.scalar.activation(
+                out=gated[i // 2][:].rearrange("p (m a b) -> p m a b", a=2, b=2)[:, queries_of(i, tiles), :, :],
+                in_=capped[i // 2][:].rearrange("p (a m b) -> p m a b", a=2, b=2)[:, queries_of(i, tiles), :, :],
+                func=ACT.Tanh)
+
         def weigh(i):
-            if i % 2 == 0:
-                w_bf[i // 2] = sbuf("w_bf%d" % i, [P, 2 * QB * PACK], BF16)
-            cols = slice(QB * PACK * (i % 2), QB * PACK * (i % 2 + 1))
             nc.vector.scalar_tensor_tensor(
-                out=w_bf[i // 2][:, cols].rearrange("p (q r) -> p q r", r=PACK),
-                in0=gated[i][:].rearrange("p (q r) -> p q r", r=PACK), scalar=1.0,
+                out=w_bf[i // 2][:].rearrange("p (m r) -> p m r", r=PACK)[:, queries_of(i), :],
+                in0=gated[i // 2][:].rearrange("p (m r) -> p m r", r=PACK)[:, queries_of(i), :], scalar=1.0,
                 in1=half_t[:, 0:PACK].unsqueeze(1).to_broadcast([P, QB, PACK]),
                 op0=ALU.add, op1=ALU.mult)
 
@@ -248,7 +252,7 @@ def tile_rows_a_sigmoid_cap_onorm_kernel(tc, qT, kT, t, v, gn, out):
         middle_sums = sum_sq_links(1, 0.0)
         small_work = early_roots + [lambda: finish(2), middle_sums[0], lambda: finish(3), middle_sums[1],
                                     lambda: finish(0)]
-        first_gap = 2 * (EARLY + 1) + 1
+        first_gap = 4 * (EARLY // 2) + 2
 
         def fill(gap):
             if 0 <= gap - first_gap < len(small_work):
@@ -257,38 +261,40 @@ def tile_rows_a_sigmoid_cap_onorm_kernel(tc, qT, kT, t, v, gn, out):
         scores(0)
         scores(1)
         scores(2, 3)
-        tanh_cap(0)
         round_v(0)
         round_q(1)
         nc.vector.tensor_scalar(out=half_t[:], in0=t_sb[:], scalar1=0.5, scalar2=None, op0=ALU.mult)
         quantize_v(0)
         quantize_q(1)
         round_v(1)
+        quantize_v(1)
 
-        last = TILES - 1
-        for i in range(last):
+        tanh_cap(0)
+        for pair in range(PAIRS):
+            i = 2 * pair
+            by_tile = pair in (0, PAIRS - 1)
             tanh_cap(i + 1)
-            if i % 2 == 0 and i + H < TILES:
-                scores(i + H, i + H + 1)
-            tanh_gate(i)
-            weigh(i)
-            fill(2 * i)
-            if i == 0:
-                quantize_v(1)
-            elif i == 1:
-                round_q(2)
-            elif i % 2 == 0:
-                mix(i // 2 - 1)
-            elif i - 3 < EARLY + MIDDLE:
-                moments((i - 3) // 2)
-            if i == 2:
-                quantize_q(2)
-            fill(2 * i + 1)
+            if by_tile:
+                tanh_gate(i, 1)
+            if i + 2 < TILES:
+                tanh_cap(i + 2)
+            tanh_gate(*((i + 1, 1) if by_tile else (i, 2)))
 
-        tanh_gate(last)
-        weigh(last)
-        finish(1)
-        mix(PAIRS - 1)
+            weigh(i)
+            fill(4 * pair)
+            if pair == 0:
+                round_q(2)
+            weigh(i + 1)
+            fill(4 * pair + 1)
+            if pair == 0:
+                quantize_q(2)
+            elif i - 2 < EARLY + MIDDLE:
+                moments(pair - 1)
+            elif pair == PAIRS - 1:
+                finish(1)
+            fill(4 * pair + 2)
+            mix(pair)
+            fill(4 * pair + 3)
 
         inverse_root(1, slice(0, MIDDLE))
         for cols in (slice(0, FINAL - 2), slice(FINAL - 2, FINAL)):

import math
from contextlib import ExitStack

import concourse.mybir as mybir

H, D, NQ, N, E = 4, 128, 512, 512, 128
FLOPS = 2 * H * N * NQ * D + 2 * H * NQ * N * E

F32 = mybir.dt.float32
BF16 = mybir.dt.bfloat16
U32 = mybir.dt.uint32
I32 = mybir.dt.int32
U8 = mybir.dt.uint8
FP8X4 = mybir.dt.float8_e4m3fn_x4
ACT = mybir.ActivationFunctionType
ALU = mybir.AluOpType

P = 128
PACK = 4
ROWS = D // PACK
QB = 128
TILES = H * NQ // QB
PAIRS = TILES // 2
KEY_HALF = N // 2
RUN = 4
EPS = 256 * 1e-5

EARLY = 4
FINAL = 6
MIDDLE = TILES - EARLY - FINAL

ROOT_GUESS = float(0x5F1FFFF9)
ROOT_STEPS = (
    (-0.703952253, 0.703952253 * 2.38924456),
    (-0.5, 1.5),
    (-0.5 * math.sqrt(E), 1.5 * math.sqrt(E)),
)


def tile_rows_a_sigmoid_cap_onorm_kernel(tc, qT, kT, t, v, gn, out):
    nc = tc.nc
    with ExitStack() as ctx:
        sb = ctx.enter_context(tc.tile_pool(name="sb", bufs=1))
        ps = ctx.enter_context(tc.psum_pool(name="ps", bufs=1))
        ctx.enter_context(tc.manual_schedule())

        def sbuf(name, shape, dtype):
            return sb.tile(shape, dtype, name=name, align_bytes=64)

        def quantize(name, src, words):
            codes = sbuf(name + "_codes", [P, words], U32)
            scales = sbuf(name + "_scales", [P, words], U8)
            nc.vector.quantize_mx(out=codes[:].bitcast(FP8X4), scales=scales[:], in_=src)
            return codes, scales

        q_hbm = qT.rearrange("h (p j) n -> (h p) j n", j=PACK)
        k_hbm = kT.rearrange("h (p j) n -> (h p) j n", j=PACK)
        v_hbm = v.rearrange("h (s r) e -> s h (r e)", r=PACK)

        q_raw = [sbuf("q_raw0", [P, PACK, QB], F32), sbuf("q_raw1", [P, PACK, QB], F32),
                 sbuf("q_raw2", [P, PACK, 2 * QB], F32)]
        k_raw = [sbuf("k_raw%d" % half, [P, PACK, KEY_HALF], F32) for half in range(2)]
        v_raw = [sbuf("v_raw%d" % g, [P, 2, PACK * E], F32) for g in range(2)]
        t_sb = sbuf("t_sb", [P, PACK], F32)
        gn_sb = sbuf("gn_sb", [P, E], F32)

        nc.sync.dma_start(out=q_raw[0][:], in_=q_hbm[:, :, 0:QB])
        for half in range(2):
            nc.sync.dma_start(out=k_raw[half][:], in_=k_hbm[:, :, half * KEY_HALF:(half + 1) * KEY_HALF])
        nc.sync.dma_start(out=v_raw[0][:], in_=v_hbm[:, 0:2, :])
        nc.sync.dma_start(out=t_sb[:], in_=t.rearrange("(s r) o -> s (r o)", r=PACK))
        nc.sync.dma_start(out=q_raw[1][:], in_=q_hbm[:, :, QB:2 * QB])
        nc.sync.dma_start(out=v_raw[1][:], in_=v_hbm[:, 2:4, :])
        nc.sync.dma_start(out=q_raw[2][:], in_=q_hbm[:, :, 2 * QB:4 * QB])
        nc.sync.dma_start(out=gn_sb[:], in_=gn)

        q_bf, q_mx, v_bf, v_mx = {}, {}, {}, {}

        def round_q(first):
            q_bf[first] = sbuf("q_bf%d" % first, [P, q_raw[first].shape[2] * PACK], BF16)
            nc.vector.tensor_copy(
                out=q_bf[first][:].rearrange("p (m x j) -> p m j x", x=RUN, j=PACK),
                in_=q_raw[first][:].rearrange("p j (m x) -> p m j x", x=RUN))

        def quantize_q(first):
            width = q_raw[first].shape[2]
            codes, scales = quantize("q%d" % first, q_bf[first][:], width)
            for c in range(width // QB):
                q_mx[first + c] = (codes[:, c * QB:(c + 1) * QB], scales[:, c * QB:(c + 1) * QB])

        def round_v(g):
            v_bf[g] = sbuf("v_bf%d" % g, [P, 2 * E * PACK], BF16)
            nc.vector.tensor_copy(
                out=v_bf[g][:].rearrange("p (u m x r) -> p u m r x", u=2, x=RUN, r=PACK),
                in_=v_raw[g][:].rearrange("p u (r m x) -> p u m r x", r=PACK, x=RUN))

        def quantize_v(g):
            v_mx[g] = quantize("v%d" % g, v_bf[g][:], 2 * E)

        round_q(0)
        quantize_q(0)

        k_codes = sbuf("k_codes", [P, N], U32)
        k_scales = sbuf("k_scales", [P, N], U8)
        half_cols = KEY_HALF // PACK
        for half in range(2):
            k_bf = [sbuf("k_bf%d%d" % (half, a), [P, 2, half_cols * PACK], BF16) for a in range(2)]
            for a, copy in enumerate((nc.vector.tensor_copy, nc.scalar.copy)):
                copy(out=k_bf[a][:].rearrange("p b (s j) -> p s j b", j=PACK),
                     in_=k_raw[half][:].rearrange("p j (s r) -> p s j r", r=PACK)[:, :, :, 2 * a:2 * a + 2])
            for r in range(PACK):
                cols = slice(P * r + half_cols * half, P * r + half_cols * (half + 1))
                nc.vector.quantize_mx(out=k_codes[:, cols].bitcast(FP8X4), scales=k_scales[:, cols],
                                      in_=k_bf[r // 2][:, r % 2, :])

        score_bank = [ps.tile([P, PACK * QB], F32, name="score%d" % h) for h in range(H)]
        y_bank = [ps.tile([P, 4 * E], F32, name="y%d" % n) for n in range(PAIRS // 2)]

        def y_of(i, tiles=1):
            pair = i // 2
            first = 2 * (pair // (PAIRS // 2)) + i % 2
            return y_bank[min(pair, PAIRS - 1 - pair)][:, first * E:(first + tiles) * E]

        def scores(*tiles):
            for r in range(PACK):
                cols = slice(P * r, P * (r + 1))
                for i in tiles:
                    c, h = divmod(i, H)
                    rows = slice(ROWS * h, ROWS * (h + 1))
                    q_codes, q_scales = q_mx[c]
                    nc.tensor.matmul_mx(
                        out=score_bank[h][:, r * QB:(r + 1) * QB],
                        lhsT=k_codes[rows, cols].bitcast(FP8X4), lhsT_scale=k_scales[rows, cols],
                        rhs=q_codes[rows, :].bitcast(FP8X4), rhs_scale=q_scales[rows, :],
                        start=True, stop=True)

        capped, gated, w_bf = {}, {}, {}
        for pair in range(PAIRS):
            capped[pair] = sbuf("capped%d" % pair, [P, 2 * QB * PACK], F32)
            gated[pair] = sbuf("gated%d" % pair, [P, 2 * QB * PACK], F32)
            w_bf[pair] = sbuf("w_bf%d" % pair, [P, 2 * QB * PACK], BF16)
        half_t = sbuf("half_t", [P, PACK], F32)

        def queries_of(i, tiles=1):
            return slice(QB * (i % 2), QB * (i % 2 + tiles))

        def tanh_cap(i):
            nc.scalar.activation(
                out=capped[i // 2][:].rearrange("p (a m b) -> p a m b", a=2, b=2)[:, :, queries_of(i), :],
                in_=score_bank[i % H][:].rearrange("p (a b q) -> p a q b", a=2, b=2),
                func=ACT.Tanh, scale=0.5)
            if i + H < TILES:
                scores(i + H)

        def tanh_gate(i, tiles):
            nc.scalar.activation(
                out=gated[i // 2][:].rearrange("p (m a b) -> p m a b", a=2, b=2)[:, queries_of(i, tiles), :, :],
                in_=capped[i // 2][:].rearrange("p (a m b) -> p m a b", a=2, b=2)[:, queries_of(i, tiles), :, :],
                func=ACT.Tanh)

        def weigh(i):
            nc.vector.scalar_tensor_tensor(
                out=w_bf[i // 2][:].rearrange("p (m r) -> p m r", r=PACK)[:, queries_of(i), :],
                in0=gated[i // 2][:].rearrange("p (m r) -> p m r", r=PACK)[:, queries_of(i), :], scalar=1.0,
                in1=half_t[:, 0:PACK].unsqueeze(1).to_broadcast([P, QB, PACK]),
                op0=ALU.add, op1=ALU.mult)

        def mix(pair):
            w_codes, w_scales = quantize("w%d" % pair, w_bf[pair][:], 2 * QB)
            v_codes, v_scales = v_mx[pair % 2]
            for u in range(2):
                cols = slice(QB * u, QB * (u + 1))
                nc.tensor.matmul_mx(
                    out=y_of(2 * pair + u), lhsT=w_codes[:, cols].bitcast(FP8X4), lhsT_scale=w_scales[:, cols],
                    rhs=v_codes[:, cols].bitcast(FP8X4), rhs_scale=v_scales[:, cols],
                    start=True, stop=True)

        sizes = (EARLY, MIDDLE, FINAL)
        stats = [sbuf("stats%d" % g, [P, 3 * sizes[g]], F32) for g in range(2)]
        mean_sq = [sbuf("mean_sq%d" % g, [P, sizes[g]], F32) for g in range(2)]
        sum_sq = [sbuf("sum_sq%d" % g, [P, sizes[g]], F32) for g in range(3)]
        inv_rms = [sbuf("inv_rms%d" % g, [P, sizes[g]], F32) for g in range(3)]

        def group_of(i):
            if i < EARLY:
                return 0, i
            if i < EARLY + MIDDLE:
                return 1, i - EARLY
            return 2, i - EARLY - MIDDLE

        def moments(pair):
            g, n = group_of(2 * pair)
            nc.vector.bn_stats(out=stats[g][:, 3 * n:3 * n + 6],
                               in_=y_of(2 * pair, 2).rearrange("p (u e) -> p e u", u=2))

        def sum_sq_links(g, addend):
            means = stats[g][:, 1:3 * sizes[g]:3]
            return [
                lambda: nc.vector.scalar_tensor_tensor(
                    out=mean_sq[g][:], in0=means, scalar=float(E), in1=means, op0=ALU.mult, op1=ALU.mult),
                lambda: nc.vector.scalar_tensor_tensor(
                    out=sum_sq[g][:], in0=stats[g][:, 2:3 * sizes[g]:3], scalar=addend, in1=mean_sq[g][:],
                    op0=ALU.add, op1=ALU.add),
            ]

        def root_step_links(n, root, better):
            root_sq = sbuf("root_sq%d" % n, [P, EARLY], F32)
            term = sbuf("term%d" % n, [P, EARLY], F32)
            factor, addend = ROOT_STEPS[n]
            return [
                lambda: nc.vector.tensor_tensor(out=root_sq[:], in0=root, in1=root, op=ALU.mult),
                lambda: nc.vector.scalar_tensor_tensor(
                    out=term[:], in0=root_sq[:], scalar=factor, in1=sum_sq[0][:], op0=ALU.mult, op1=ALU.mult),
                lambda: nc.vector.scalar_tensor_tensor(
                    out=better, in0=term[:], scalar=addend, in1=root, op0=ALU.add, op1=ALU.mult),
            ]

        guess = sbuf("guess", [P, EARLY], I32)
        early_roots = sum_sq_links(0, E * EPS)
        early_roots.append(lambda: nc.vector.tensor_scalar(
            out=guess[:], in0=sum_sq[0][:].bitcast(I32), scalar1=-0.5, scalar2=ROOT_GUESS,
            op0=ALU.mult, op1=ALU.add))
        roots = [guess[:].bitcast(F32)]
        for n in range(len(ROOT_STEPS) - 1):
            roots.append(sbuf("root%d" % n, [P, EARLY], F32)[:])
        roots.append(inv_rms[0][:])
        for n in range(len(ROOT_STEPS)):
            early_roots.extend(root_step_links(n, roots[n], roots[n + 1]))

        squares = sbuf("squares", [P, E], F32)

        def sum_squares(i):
            g, n = group_of(i)
            nc.scalar.activation(out=squares[:], in_=y_of(i), func=ACT.Square, accum_out=sum_sq[g][:, n:n + 1])

        def inverse_root(g, cols):
            nc.scalar.activation(out=inv_rms[g][:, cols], in_=sum_sq[g][:, cols], func=ACT.Abs_reciprocal_sqrt,
                                 scale=1.0 / E, bias=EPS)

        result = [sbuf("result%d" % pair, [P, 2, E], F32) for pair in range(PAIRS)]

        def finish(i):
            g, n = group_of(i)
            nc.vector.scalar_tensor_tensor(
                out=result[i // 2][:, i % 2, :], in0=y_of(i), scalar=inv_rms[g][:, n:n + 1], in1=gn_sb[:],
                op0=ALU.mult, op1=ALU.mult)
            if i % 2 == 1:
                c, h = divmod(i - 1, H)
                nc.sync.dma_start(out=out[h:h + 2, c * QB:(c + 1) * QB, :].rearrange("h q e -> q h e"),
                                  in_=result[i // 2][:])

        middle_sums = sum_sq_links(1, 0.0)
        small_work = early_roots + [lambda: finish(2), middle_sums[0], lambda: finish(3), middle_sums[1],
                                    lambda: finish(0)]
        first_gap = 4 * (EARLY // 2) + 2

        def fill(gap):
            if 0 <= gap - first_gap < len(small_work):
                small_work[gap - first_gap]()

        scores(0)
        scores(1)
        scores(2, 3)
        round_v(0)
        round_q(1)
        nc.vector.tensor_scalar(out=half_t[:], in0=t_sb[:], scalar1=0.5, scalar2=None, op0=ALU.mult)
        quantize_v(0)
        quantize_q(1)
        round_v(1)
        quantize_v(1)

        tanh_cap(0)
        for pair in range(PAIRS):
            i = 2 * pair
            by_tile = pair in (0, PAIRS - 1)
            tanh_cap(i + 1)
            if by_tile:
                tanh_gate(i, 1)
            if i + 2 < TILES:
                tanh_cap(i + 2)
            tanh_gate(*((i + 1, 1) if by_tile else (i, 2)))

            weigh(i)
            fill(4 * pair)
            if pair == 0:
                round_q(2)
            weigh(i + 1)
            fill(4 * pair + 1)
            if pair == 0:
                quantize_q(2)
            elif i - 2 < EARLY + MIDDLE:
                moments(pair - 1)
            elif pair == PAIRS - 1:
                finish(1)
            fill(4 * pair + 2)
            mix(pair)
            fill(4 * pair + 3)

        inverse_root(1, slice(0, MIDDLE))
        for cols in (slice(0, FINAL - 2), slice(FINAL - 2, FINAL)):
            for n in range(cols.start, cols.stop):
                sum_squares(EARLY + MIDDLE + n)
            inverse_root(2, cols)

        for pair in (3, 4, 2, 5, 6, 7):
            finish(2 * pair)
            finish(2 * pair + 1)
